import numpy as np
import ml_dtypes


def mxq(x, axis, fmt="e4m3"):
    dtype, down = {"e4m3": (ml_dtypes.float8_e4m3fn, 7), "e5m2": (ml_dtypes.float8_e5m2, 14)}[fmt]
    v = np.moveaxis(np.asarray(x, np.float32).astype(ml_dtypes.bfloat16).astype(np.float64), axis, -1)
    blocks = v.reshape(v.shape[:-1] + (-1, 32))
    amax = np.abs(blocks).max(-1, keepdims=True)
    byte = np.maximum(np.where(amax > 0, np.frexp(amax)[1] - 1 + 127, 0) - down, 1)
    scale = np.exp2(byte - 127.0)
    codes = (blocks / scale).astype(np.float32).astype(dtype).astype(np.float64)
    return np.moveaxis((codes * scale).reshape(v.shape), -1, axis)


WIDE = False


def mx_kscale(k):
    if not WIDE:
        return np.ones(k)
    levels = np.array([10, -10, 5, -5, 0])
    if k % 512:
        return np.exp2(np.random.permutation(np.resize(levels, k // 32))).repeat(32)
    a = np.empty((k // 512, 16))
    for p in range(k // 512):
        a[p, :8] = np.random.permutation(np.resize(levels, 8))
        for g in range(8):
            far = levels[np.abs(levels - a[p, g]) >= 10]
            a[p, g + 8] = far[np.random.randint(len(far))]
    return np.exp2(a.ravel()).repeat(32)


def f64(x):
    return np.asarray(x).astype(np.float64)


def striped(idx):
    return np.tile(idx.reshape(-1, 16).T, (8, 1)).astype(np.uint16)


def unstriped(offs):
    return offs[:16].T.reshape(-1).astype(np.int64)


E2M1 = np.array([0.0, 0.5, 1.0, 1.5, 2.0, 3.0, 4.0, 6.0, -0.0, -0.5, -1.0, -1.5, -2.0, -3.0, -4.0, -6.0])


def pack_weight(w, fmt):
    k, n = w.shape
    w = f64(np.asarray(w, np.float32).astype(ml_dtypes.bfloat16)).reshape(k // 32, 32, n)
    amax = np.abs(w).max(1)
    if fmt == "e4m3":
        byte = np.frexp(amax)[1] - 1 + 127 - 7
    else:
        mant, ex = np.frexp(amax / 6.0)
        byte = np.where(mant > 0.5, ex, ex - 1) + 127
    byte = np.clip(np.where(amax > 0, byte, 1), 1, 254)
    scaled = (w * np.exp2(127.0 - byte)[:, None, :]).reshape(k, n).astype(np.float32)
    by_word = np.ascontiguousarray(scaled.reshape(k // 512, 128, 4, n).transpose(0, 1, 3, 2))
    if fmt == "e4m3":
        words = by_word.astype(ml_dtypes.float8_e4m3fn).view(np.uint8)
    else:
        c = by_word.astype(ml_dtypes.float4_e2m1fn).view(np.uint8) & 0xF
        words = (c[..., 0::2] | (c[..., 1::2] << 4)).reshape(k // 512, 128, 2 * n)
    return np.ascontiguousarray(words), np.ascontiguousarray(byte.astype(np.uint8).reshape(k // 512, 16, n))


def unpack_weight(words, scales, fmt):
    g, _, n = scales.shape
    words = np.ascontiguousarray(words).reshape(g, 128, n, -1)
    if fmt == "e4m3":
        vals = words.view(ml_dtypes.float8_e4m3fn).astype(np.float64)
    else:
        nib = np.empty((g, 128, n, 4), np.uint8)
        nib[..., 0::2] = words & 0xF
        nib[..., 1::2] = words >> 4
        vals = E2M1[nib]
    vals = vals * np.repeat(np.exp2(scales.astype(np.float64) - 127.0), 8, axis=1)[..., None]
    return vals.transpose(0, 1, 3, 2).reshape(g * 512, n)


def relu2(v):
    return np.maximum(v, 0.0) ** 2


K, T, E, C, H, N = 2048, 512, 6, 128, 512, 384
R = 4


def by_expert(wq, xq):
    return np.concatenate([wq[e].T @ xq[:, e * C:(e + 1) * C] for e in range(E)], axis=1)


def setup_inputs():
    n = np.random.standard_normal
    s = mx_kscale(K)[:, None]
    u = mx_kscale(H)
    slot_token = np.concatenate([r * (T // R) + np.random.permutation(T // R)[:C // R] for e in range(E) for r in range(R)])
    w1 = [pack_weight(m, "e2m1") for m in n((E, K, H)) / np.sqrt(K) / s[None] * u[None, None, :]]
    w2 = [pack_weight(m, "e2m1") for m in n((E, H, N)) / np.sqrt(H) / u[None, :, None] ** 2]
    return {
        "xT": (n((K, T)) * s).astype(np.float32),
        "w1_words": np.stack([m[0] for m in w1]),
        "w1_scales": np.stack([m[1] for m in w1]),
        "w2_words": np.stack([m[0] for m in w2]),
        "w2_scales": np.stack([m[1] for m in w2]),
        "offs": striped(slot_token),
    }


def reference(xT, w1_words, w1_scales, w2_words, w2_scales, offs):
    idx = unstriped(offs)
    w1 = np.stack([unpack_weight(w1_words[e], w1_scales[e], "e2m1") for e in range(E)])
    w2 = np.stack([unpack_weight(w2_words[e], w2_scales[e], "e2m1") for e in range(E)])
    xq = mxq(f64(xT)[:, idx], 0, "e4m3")
    h = relu2(by_expert(w1, xq))
    y = by_expert(w2, mxq(h, 0, "e4m3"))
    return y.reshape(N, E, R, C // R).transpose(0, 2, 1, 3).reshape(N, E * C)

@@ -1,0 +1,223 @@
+from contextlib import ExitStack
+
+import concourse.mybir as mybir
+from concourse.masks import make_identity
+
+K, T, E, C, H, N, R = 2048, 512, 6, 128, 512, 384, 4
+P = 128
+S = K // 512
+SLOTS = E * C
+FLOPS = 2 * SLOTS * (K * H + H * N)
+
+F32 = mybir.dt.float32
+BF16 = mybir.dt.bfloat16
+U32 = mybir.dt.uint32
+I32 = mybir.dt.int32
+U16 = mybir.dt.uint16
+U8 = mybir.dt.uint8
+E4M3 = mybir.dt.float8_e4m3fn_x4
+E2M1 = mybir.dt.float4_e2m1fn_x4
+RELU = mybir.ActivationFunctionType.Relu
+SQUARE = mybir.ActivationFunctionType.Square
+
+
+def tile_moe_eps_mlp_relu2_kernel(
+    tc, xT, w1_words, w1_scales, w2_words, w2_scales, offs, out
+):
+    nc = tc.nc
+    with ExitStack() as ctx:
+        keep = ctx.enter_context(tc.tile_pool(name="keep", bufs=1))
+        work = ctx.enter_context(tc.tile_pool(name="work", bufs=3))
+        psum_a = ctx.enter_context(tc.psum_pool(name="psum_a", bufs=4))
+        psum_t = ctx.enter_context(tc.psum_pool(name="psum_t", bufs=2))
+        psum_y = ctx.enter_context(tc.psum_pool(name="psum_y", bufs=2))
+
+        offsets = keep.tile([P, SLOTS // 16], U16, name="offsets")
+        x = [keep.tile([P, 4, T], F32, name=f"x{s}") for s in range(S)]
+        xg = [keep.tile([P, T, 4], BF16, name=f"xg{s}", align_bytes=64) for s in range(S)]
+        codes = [keep.tile([P, T], U32, name=f"codes{s}", align_bytes=64) for s in range(S)]
+        scales = [keep.tile([P, T], U8, name=f"scales{i}", align_bytes=64) for i in range(S)]
+        gcodes = [keep.tile([P, SLOTS], U32, name=f"gcodes{s}", align_bytes=64) for s in range(S)]
+        gscales = [keep.tile([P, SLOTS], U8, name=f"gscales{s}", align_bytes=64) for s in range(S)]
+        w1 = [keep.tile([P, S, 2 * H], U8, name=f"w1_{e}", align_bytes=64) for e in range(E)]
+        w1s = keep.tile([P, E * S, H], U8, name="w1s", align_bytes=64)
+        w2 = keep.tile([P, E, 2 * N], U8, name="w2", align_bytes=64)
+        w2s = keep.tile([P, E, N], U8, name="w2s", align_bytes=64)
+        y = keep.tile([P, N // P, R, E, C // R], F32, name="y", align_bytes=64)
+        ident = keep.tile([P, P], F32, name="ident", align_bytes=64)
+
+        def load_x(s, c0, c1):
+            rows = xT[512 * s : 512 * (s + 1), c0:c1].rearrange("(p j) w -> p j w", j=4)
+            nc.sync.dma_start(out=x[s][:, :, c0:c1], in_=rows)
+
+        load_x(0, 0, 256)
+        nc.sync.dma_start(offsets[:], offs)
+        load_x(0, 256, 512)
+        load_x(1, 0, T)
+        load_x(2, 0, T)
+
+        nc.vector.memset(w1s[:].rearrange("p a i -> p (a i)").bitcast(I32), 0)
+        nc.vector.memset(w2s[:].rearrange("p a i -> p (a i)").bitcast(I32), 0)
+        for s in range(S):
+            nc.gpsimd.memset(scales[s][:], 0)
+        make_identity(nc, ident[:])
+
+        def load_w1s(e0, e1):
+            for r in range(4):
+                nc.sync.dma_start(
+                    out=w1s[r:P:32, S * e0 : S * e1, :].bitcast(I32),
+                    in_=w1_scales[e0:e1].rearrange("e s (b r) i -> r b (e s) i", r=4)[r].bitcast(I32),
+                )
+
+        def load_w1(e):
+            nc.sync.dma_start(
+                out=w1[e][:].bitcast(I32),
+                in_=w1_words[e].rearrange("s p b -> p s b").bitcast(I32),
+            )
+
+        load_w1s(0, 3)
+        load_w1(0)
+        load_x(3, 0, 512)
+        load_w1(1)
+        load_w1(2)
+        load_w1s(3, 6)
+        load_w1(3)
+        load_w1(4)
+        load_w1(5)
+        for r in range(4):
+            nc.sync.dma_start(
+                out=w2s[r:P:32, :, :].bitcast(I32),
+                in_=w2_scales.rearrange("e s (b r) i -> r b (e s) i", r=4)[r].bitcast(I32),
+            )
+        nc.sync.dma_start(
+            out=w2[:].bitcast(I32),
+            in_=w2_words.rearrange("e s p b -> p (e s) b").bitcast(I32),
+        )
+
+        def cast(copy, s, c0, c1):
+            copy(
+                out=xg[s][:, c0:c1, :].rearrange("p (c i) j -> p c j i", i=4),
+                in_=x[s][:, :, c0:c1].rearrange("p j (c i) -> p c j i", i=4),
+            )
+
+        def quantize(s):
+            nc.vector.quantize_mx(
+                out=codes[s][:].bitcast(E4M3),
+                scales=scales[s][:],
+                in_=xg[s][:].rearrange("p w j -> p (w j)"),
+            )
+
+        def gather(s, j0, j1):
+            entries = offsets[:, j0 // 16 : j1 // 16]
+            nc.vector.tensor_copy(gcodes[s][:, j0:j1], codes[s][:].indirect(entries))
+
+        def gather_scales(s, j0, j1):
+            entries = offsets[:, j0 // 16 : j1 // 16]
+            nc.vector.tensor_copy(gscales[s][:, j0:j1], scales[s][:].indirect(entries))
+
+        cast(nc.scalar.copy, 0, 0, 256)
+        cast(nc.vector.tensor_copy, 0, 256, 384)
+        cast(nc.scalar.copy, 0, 384, 512)
+        for s in range(1, S):
+            for c0 in (0, 256):
+                cast(nc.scalar.copy, s, c0, c0 + 256)
+        for s in range(S):
+            quantize(s)
+            if s < S - 1:
+                for j0, j1 in ((0, 384), (384, 768)):
+                    gather(s, j0, j1)
+                    gather_scales(s, j0, j1)
+
+        def first(e):
+            a = psum_a.tile([P, H], F32, name="a")
+            cols = slice(C * e, C * (e + 1))
+            for s in range(S):
+                nc.tensor.matmul_mx(
+                    out=a[:],
+                    lhsT=gcodes[s][:, cols].bitcast(E4M3),
+                    lhsT_scale=gscales[s][:, cols],
+                    rhs=w1[e][:, s, :].bitcast(E2M1),
+                    rhs_scale=w1s[:, S * e + s, :],
+                    start=(s == 0),
+                    stop=(s == S - 1),
+                )
+            return a
+
+        def relu(e, a):
+            r = work.tile([P, 4, P], F32, name="r", align_bytes=64)
+            src = a[:].rearrange("c (p t) -> c t p", t=4)
+            if e < 3:
+                nc.scalar.activation(r[:], src, RELU)
+            else:
+                nc.vector.tensor_scalar_max(r[:], src, 0.0)
+            return r
+
+        def turn(r):
+            t = psum_t.tile([P, 4, C], F32, name="t")
+            for d in range(4):
+                nc.tensor.transpose(t[:, d, :], r[:, d, :], ident[:])
+            return t
+
+        def square(t):
+            h = work.tile([P, C, 4], BF16, name="h", align_bytes=64)
+            nc.scalar.activation(h[:], t[:].rearrange("p t c -> p c t"), SQUARE)
+            return h
+
+        def quantize_h(h):
+            hc = work.tile([P, C], U32, name="hc", align_bytes=64)
+            hs = work.tile([P, C], U8, name="hs", align_bytes=64)
+            nc.vector.quantize_mx(out=hc[:].bitcast(E4M3), scales=hs[:], in_=h[:].rearrange("p c t -> p (c t)"))
+            return hc, hs
+
+        def second(e, hc, hs):
+            b = psum_y.tile([P, N // P, C], F32, name="b")
+            for n in range(N // P):
+                nc.tensor.matmul_mx(
+                    out=b[:, n, :],
+                    lhsT=w2[:, e, 2 * P * n : 2 * P * (n + 1)].bitcast(E2M1),
+                    lhsT_scale=w2s[:, e, P * n : P * (n + 1)],
+                    rhs=hc[:].bitcast(E4M3),
+                    rhs_scale=hs[:],
+                    start=True,
+                    stop=True,
+                )
+            return b
+
+        def collect(e, b):
+            dst = y[:, :, :, e, :]
+            src = b[:].rearrange("p n (m u) -> p n m u", m=R)
+            if e >= 3:
+                nc.vector.tensor_copy(dst, src)
+            else:
+                nc.scalar.copy(dst, src)
+
+        def store(e0, e1):
+            view = out.rearrange("(n p) (m e u) -> p n m e u", p=P, m=R, e=E)
+            for n in range(N // P):
+                nc.sync.dma_start(
+                    out=view[:, n, :, e0:e1, :].rearrange("p m e u -> p m (e u)"),
+                    in_=y[:, n, :, e0:e1, :].rearrange("p m e u -> p m (e u)"),
+                )
+
+        a, r, t, q, b = {}, {}, {}, {}, {}
+        for i in range(E + 2):
+            if i < E:
+                gather(S - 1, C * i, C * (i + 1))
+                gather_scales(S - 1, C * i, C * (i + 1))
+                a[i] = first(i)
+            if 0 <= i - 1 < E:
+                t[i - 1] = turn(r[i - 1])
+            if 0 <= i - 2 < E:
+                b[i - 2] = second(i - 2, *q[i - 2])
+            if i < E:
+                r[i] = relu(i, a[i])
+            if 0 <= i - 1 < E:
+                h = square(t[i - 1])
+                q[i - 1] = quantize_h(h)
+            if 0 <= i - 2 < E:
+                collect(i - 2, b[i - 2])
+            if i - 2 == 2:
+                store(0, 3)
+            if i - 2 == 4:
+                store(3, 5)
+        store(5, 6)

@@ -36,7 +36,7 @@ def tile_moe_eps_mlp_relu2_kernel(
         x = [keep.tile([P, 4, T], F32, name=f"x{s}") for s in range(S)]
         xg = [keep.tile([P, T, 4], BF16, name=f"xg{s}", align_bytes=64) for s in range(S)]
         codes = [keep.tile([P, T], U32, name=f"codes{s}", align_bytes=64) for s in range(S)]
-        scales = [keep.tile([P, T], U8, name=f"scales{i}", align_bytes=64) for i in range(S)]
+        scales = [keep.tile([P, T], U8, name=f"scales{i}", align_bytes=64) for i in range(3)]
         gcodes = [keep.tile([P, SLOTS], U32, name=f"gcodes{s}", align_bytes=64) for s in range(S)]
         gscales = [keep.tile([P, SLOTS], U8, name=f"gscales{s}", align_bytes=64) for s in range(S)]
         w1 = [keep.tile([P, S, 2 * H], U8, name=f"w1_{e}", align_bytes=64) for e in range(E)]
@@ -55,18 +55,20 @@ def tile_moe_eps_mlp_relu2_kernel(
         load_x(0, 256, 512)
         load_x(1, 0, T)
         load_x(2, 0, T)
+        load_x(3, 0, T)
 
-        nc.vector.memset(w1s[:].rearrange("p a i -> p (a i)").bitcast(I32), 0)
+        for i in range(3):
+            nc.gpsimd.memset(scales[i][:], 0)
+        nc.gpsimd.memset(gscales[1][:], 0)
+        nc.gpsimd.memset(w1s[:].rearrange("p a i -> p (a i)").bitcast(I32), 0)
         nc.vector.memset(w2s[:].rearrange("p a i -> p (a i)").bitcast(I32), 0)
-        for s in range(S):
-            nc.gpsimd.memset(scales[s][:], 0)
         make_identity(nc, ident[:])
 
-        def load_w1s(e0, e1):
+        def load_w1s():
             for r in range(4):
-                nc.sync.dma_start(
-                    out=w1s[r:P:32, S * e0 : S * e1, :].bitcast(I32),
-                    in_=w1_scales[e0:e1].rearrange("e s (b r) i -> r b (e s) i", r=4)[r].bitcast(I32),
+                nc.gpsimd.dma_start(
+                    out=w1s[r:P:32, :, :].bitcast(I32),
+                    in_=w1_scales.rearrange("e s (b r) i -> r b (e s) i", r=4)[r].bitcast(I32),
                 )
 
         def load_w1(e):
@@ -75,25 +77,8 @@ def tile_moe_eps_mlp_relu2_kernel(
                 in_=w1_words[e].rearrange("s p b -> p s b").bitcast(I32),
             )
 
-        load_w1s(0, 3)
         load_w1(0)
-        load_x(3, 0, 512)
-        load_w1(1)
-        load_w1(2)
-        load_w1s(3, 6)
-        load_w1(3)
-        load_w1(4)
-        load_w1(5)
-        for r in range(4):
-            nc.sync.dma_start(
-                out=w2s[r:P:32, :, :].bitcast(I32),
-                in_=w2_scales.rearrange("e s (b r) i -> r b (e s) i", r=4)[r].bitcast(I32),
-            )
-        nc.sync.dma_start(
-            out=w2[:].bitcast(I32),
-            in_=w2_words.rearrange("e s p b -> p (e s) b").bitcast(I32),
-        )
-
+        load_w1s()
         def cast(copy, s, c0, c1):
             copy(
                 out=xg[s][:, c0:c1, :].rearrange("p (c i) j -> p c j i", i=4),
@@ -103,7 +88,7 @@ def tile_moe_eps_mlp_relu2_kernel(
         def quantize(s):
             nc.vector.quantize_mx(
                 out=codes[s][:].bitcast(E4M3),
-                scales=scales[s][:],
+                scales=(scales[0][4 * s : P, :] if s < 2 else scales[s - 1][:]),
                 in_=xg[s][:].rearrange("p w j -> p (w j)"),
             )
 
@@ -113,7 +98,7 @@ def tile_moe_eps_mlp_relu2_kernel(
 
         def gather_scales(s, j0, j1):
             entries = offsets[:, j0 // 16 : j1 // 16]
-            nc.vector.tensor_copy(gscales[s][:, j0:j1], scales[s][:].indirect(entries))
+            nc.vector.tensor_copy(gscales[s][:, j0:j1], scales[max(s - 1, 0)][:].indirect(entries))
 
         cast(nc.scalar.copy, 0, 0, 256)
         cast(nc.vector.tensor_copy, 0, 256, 384)
@@ -123,10 +108,37 @@ def tile_moe_eps_mlp_relu2_kernel(
                 cast(nc.scalar.copy, s, c0, c0 + 256)
         for s in range(S):
             quantize(s)
+            halves = ((0, 384), (384, 768))
+            if s == 1:
+                for j0, j1 in halves:
+                    gather_scales(0, j0, j1)
+                nc.scalar.dma_start(
+                    out=gscales[1][0:112, :].bitcast(I32),
+                    in_=gscales[0][4 : 4 + 112, :].bitcast(I32),
+                )
             if s < S - 1:
-                for j0, j1 in ((0, 384), (384, 768)):
+                for j0, j1 in halves:
                     gather(s, j0, j1)
-                    gather_scales(s, j0, j1)
+                    if s == 2:
+                        gather_scales(s, j0, j1)
+
+        def load_w2(e0, e1):
+            nc.sync.dma_start(
+                out=w2[:, e0:e1, :].bitcast(I32),
+                in_=w2_words[e0:e1].rearrange("e s p b -> p (e s) b").bitcast(I32),
+            )
+
+        for r in range(4):
+            nc.gpsimd.dma_start(
+                out=w2s[r:P:32, :, :].bitcast(I32),
+                in_=w2_scales.rearrange("e s (b r) i -> r b (e s) i", r=4)[r].bitcast(I32),
+            )
+        load_w1(1)
+        load_w1(2)
+        load_w1(3)
+        load_w2(0, 6)
+        load_w1(4)
+        load_w1(5)
 
         def first(e):
             a = psum_a.tile([P, H], F32, name="a")
@@ -146,7 +158,7 @@ def tile_moe_eps_mlp_relu2_kernel(
         def relu(e, a):
             r = work.tile([P, 4, P], F32, name="r", align_bytes=64)
             src = a[:].rearrange("c (p t) -> c t p", t=4)
-            if e < 3:
+            if e < 4:
                 nc.scalar.activation(r[:], src, RELU)
             else:
                 nc.vector.tensor_scalar_max(r[:], src, 0.0)
@@ -186,10 +198,7 @@ def tile_moe_eps_mlp_relu2_kernel(
         def collect(e, b):
             dst = y[:, :, :, e, :]
             src = b[:].rearrange("p n (m u) -> p n m u", m=R)
-            if e >= 3:
-                nc.vector.tensor_copy(dst, src)
-            else:
-                nc.scalar.copy(dst, src)
+            nc.vector.tensor_copy(dst, src)
 
         def store(e0, e1):
             view = out.rearrange("(n p) (m e u) -> p n m e u", p=P, m=R, e=E)

@@ -57,16 +57,14 @@ def tile_moe_eps_mlp_relu2_kernel(
         load_x(2, 0, T)
         load_x(3, 0, T)
 
-        for i in range(3):
-            nc.gpsimd.memset(scales[i][:], 0)
-        nc.gpsimd.memset(gscales[1][:], 0)
-        nc.gpsimd.memset(w1s[:].rearrange("p a i -> p (a i)").bitcast(I32), 0)
-        nc.vector.memset(w2s[:].rearrange("p a i -> p (a i)").bitcast(I32), 0)
-        make_identity(nc, ident[:])
+        nc.vector.memset(w1s[:].rearrange("p a i -> p (a i)").bitcast(I32), 0)
+        for plane in scales + [gscales[1]]:
+            nc.gpsimd.memset(plane[:], 0)
+        nc.gpsimd.memset(w2s[:].rearrange("p a i -> p (a i)").bitcast(I32), 0)
 
         def load_w1s():
             for r in range(4):
-                nc.gpsimd.dma_start(
+                nc.sync.dma_start(
                     out=w1s[r:P:32, :, :].bitcast(I32),
                     in_=w1_scales.rearrange("e s (b r) i -> r b (e s) i", r=4)[r].bitcast(I32),
                 )
@@ -79,6 +77,7 @@ def tile_moe_eps_mlp_relu2_kernel(
 
         load_w1(0)
         load_w1s()
+        make_identity(nc, ident[:])
         def cast(copy, s, c0, c1):
             copy(
                 out=xg[s][:, c0:c1, :].rearrange("p (c i) j -> p c j i", i=4),
@@ -100,27 +99,39 @@ def tile_moe_eps_mlp_relu2_kernel(
             entries = offsets[:, j0 // 16 : j1 // 16]
             nc.vector.tensor_copy(gscales[s][:, j0:j1], scales[max(s - 1, 0)][:].indirect(entries))
 
-        cast(nc.scalar.copy, 0, 0, 256)
-        cast(nc.vector.tensor_copy, 0, 256, 384)
-        cast(nc.scalar.copy, 0, 384, 512)
-        for s in range(1, S):
-            for c0 in (0, 256):
-                cast(nc.scalar.copy, s, c0, c0 + 256)
+        for s in range(S):
+            if s == 0:
+                cast(nc.scalar.copy, s, 0, 256)
+                cast(nc.vector.tensor_copy, s, 256, 384)
+                cast(nc.scalar.copy, s, 384, 512)
+            else:
+                cast(nc.scalar.copy, s, 0, 192)
+                cast(nc.scalar.copy, s, 192, 384)
+                cast(nc.vector.tensor_copy, s, 384, 512)
+
+        def gather_early(s, j0, j1):
+            if s == 1:
+                gather_scales(0, j0, j1)
+                nc.scalar.dma_start(
+                    out=gscales[1][0:112, j0:j1].bitcast(I32),
+                    in_=gscales[0][4 : 4 + 112, j0:j1].bitcast(I32),
+                )
+            gather(s, j0, j1)
+            if s == 2:
+                gather_scales(s, j0, j1)
+
+        def gather_last(e):
+            gather(S - 1, C * e, C * (e + 1))
+            gather_scales(S - 1, C * e, C * (e + 1))
+
         for s in range(S):
             quantize(s)
-            halves = ((0, 384), (384, 768))
-            if s == 1:
-                for j0, j1 in halves:
-                    gather_scales(0, j0, j1)
-                nc.scalar.dma_start(
-                    out=gscales[1][0:112, :].bitcast(I32),
-                    in_=gscales[0][4 : 4 + 112, :].bitcast(I32),
-                )
             if s < S - 1:
-                for j0, j1 in halves:
-                    gather(s, j0, j1)
-                    if s == 2:
-                        gather_scales(s, j0, j1)
+                gather_early(s, 0, 384)
+        for e in range(3):
+            gather_last(e)
+        for s in range(S - 1):
+            gather_early(s, 384, 768)
 
         def load_w2(e0, e1):
             nc.sync.dma_start(
@@ -128,15 +139,15 @@ def tile_moe_eps_mlp_relu2_kernel(
                 in_=w2_words[e0:e1].rearrange("e s p b -> p (e s) b").bitcast(I32),
             )
 
+        load_w1(1)
+        load_w1(2)
         for r in range(4):
-            nc.gpsimd.dma_start(
+            nc.sync.dma_start(
                 out=w2s[r:P:32, :, :].bitcast(I32),
                 in_=w2_scales.rearrange("e s (b r) i -> r b (e s) i", r=4)[r].bitcast(I32),
             )
-        load_w1(1)
-        load_w1(2)
-        load_w1(3)
         load_w2(0, 6)
+        load_w1(3)
         load_w1(4)
         load_w1(5)
 
@@ -211,8 +222,8 @@ def tile_moe_eps_mlp_relu2_kernel(
         a, r, t, q, b = {}, {}, {}, {}, {}
         for i in range(E + 2):
             if i < E:
-                gather(S - 1, C * i, C * (i + 1))
-                gather_scales(S - 1, C * i, C * (i + 1))
+                if i >= 3:
+                    gather_last(i)
                 a[i] = first(i)
             if 0 <= i - 1 < E:
                 t[i - 1] = turn(r[i - 1])

from contextlib import ExitStack

import concourse.mybir as mybir
from concourse.masks import make_identity

K, T, E, C, H, N, R = 2048, 512, 6, 128, 512, 384, 4
P = 128
S = K // 512
SLOTS = E * C
FLOPS = 2 * SLOTS * (K * H + H * N)

F32 = mybir.dt.float32
BF16 = mybir.dt.bfloat16
U32 = mybir.dt.uint32
I32 = mybir.dt.int32
U16 = mybir.dt.uint16
U8 = mybir.dt.uint8
E4M3 = mybir.dt.float8_e4m3fn_x4
E2M1 = mybir.dt.float4_e2m1fn_x4
RELU = mybir.ActivationFunctionType.Relu
SQUARE = mybir.ActivationFunctionType.Square


def tile_moe_eps_mlp_relu2_kernel(
    tc, xT, w1_words, w1_scales, w2_words, w2_scales, offs, out
):
    nc = tc.nc
    with ExitStack() as ctx:
        keep = ctx.enter_context(tc.tile_pool(name="keep", bufs=1))
        work = ctx.enter_context(tc.tile_pool(name="work", bufs=3))
        psum_a = ctx.enter_context(tc.psum_pool(name="psum_a", bufs=4))
        psum_t = ctx.enter_context(tc.psum_pool(name="psum_t", bufs=2))
        psum_y = ctx.enter_context(tc.psum_pool(name="psum_y", bufs=2))

        offsets = keep.tile([P, SLOTS // 16], U16, name="offsets")
        x = [keep.tile([P, 4, T], F32, name=f"x{s}") for s in range(S)]
        xg = [keep.tile([P, T, 4], BF16, name=f"xg{s}", align_bytes=64) for s in range(S)]
        codes = [keep.tile([P, T], U32, name=f"codes{s}", align_bytes=64) for s in range(S)]
        scales = [keep.tile([P, T], U8, name=f"scales{i}", align_bytes=64) for i in range(3)]
        gcodes = [keep.tile([P, SLOTS], U32, name=f"gcodes{s}", align_bytes=64) for s in range(S)]
        gscales = [keep.tile([P, SLOTS], U8, name=f"gscales{s}", align_bytes=64) for s in range(S)]
        w1 = [keep.tile([P, S, 2 * H], U8, name=f"w1_{e}", align_bytes=64) for e in range(E)]
        w1s = keep.tile([P, E * S, H], U8, name="w1s", align_bytes=64)
        w2 = keep.tile([P, E, 2 * N], U8, name="w2", align_bytes=64)
        w2s = keep.tile([P, E, N], U8, name="w2s", align_bytes=64)
        y = keep.tile([P, N // P, R, E, C // R], F32, name="y", align_bytes=64)
        ident = keep.tile([P, P], F32, name="ident", align_bytes=64)

        def load_x(s, c0, c1):
            rows = xT[512 * s : 512 * (s + 1), c0:c1].rearrange("(p j) w -> p j w", j=4)
            nc.sync.dma_start(out=x[s][:, :, c0:c1], in_=rows)

        load_x(0, 0, 256)
        nc.sync.dma_start(offsets[:], offs)
        load_x(0, 256, 512)
        load_x(1, 0, T)
        load_x(2, 0, T)
        load_x(3, 0, T)

        nc.vector.memset(w1s[:].rearrange("p a i -> p (a i)").bitcast(I32), 0)
        for plane in scales + [gscales[1]]:
            nc.gpsimd.memset(plane[:], 0)
        nc.gpsimd.memset(w2s[:].rearrange("p a i -> p (a i)").bitcast(I32), 0)

        def load_w1s():
            for r in range(4):
                nc.sync.dma_start(
                    out=w1s[r:P:32, :, :].bitcast(I32),
                    in_=w1_scales.rearrange("e s (b r) i -> r b (e s) i", r=4)[r].bitcast(I32),
                )

        def load_w1(e):
            nc.sync.dma_start(
                out=w1[e][:].bitcast(I32),
                in_=w1_words[e].rearrange("s p b -> p s b").bitcast(I32),
            )

        load_w1(0)
        load_w1s()
        make_identity(nc, ident[:])
        def cast(copy, s, c0, c1):
            copy(
                out=xg[s][:, c0:c1, :].rearrange("p (c i) j -> p c j i", i=4),
                in_=x[s][:, :, c0:c1].rearrange("p j (c i) -> p c j i", i=4),
            )

        def quantize(s):
            nc.vector.quantize_mx(
                out=codes[s][:].bitcast(E4M3),
                scales=(scales[0][4 * s : P, :] if s < 2 else scales[s - 1][:]),
                in_=xg[s][:].rearrange("p w j -> p (w j)"),
            )

        def gather(s, j0, j1):
            entries = offsets[:, j0 // 16 : j1 // 16]
            nc.vector.tensor_copy(gcodes[s][:, j0:j1], codes[s][:].indirect(entries))

        def gather_scales(s, j0, j1):
            entries = offsets[:, j0 // 16 : j1 // 16]
            nc.vector.tensor_copy(gscales[s][:, j0:j1], scales[max(s - 1, 0)][:].indirect(entries))

        for s in range(S):
            if s == 0:
                cast(nc.scalar.copy, s, 0, 256)
                cast(nc.vector.tensor_copy, s, 256, 384)
                cast(nc.scalar.copy, s, 384, 512)
            else:
                cast(nc.scalar.copy, s, 0, 192)
                cast(nc.scalar.copy, s, 192, 384)
                cast(nc.vector.tensor_copy, s, 384, 512)

        def gather_early(s, j0, j1):
            if s == 1:
                gather_scales(0, j0, j1)
                nc.scalar.dma_start(
                    out=gscales[1][0:112, j0:j1].bitcast(I32),
                    in_=gscales[0][4 : 4 + 112, j0:j1].bitcast(I32),
                )
            gather(s, j0, j1)
            if s == 2:
                gather_scales(s, j0, j1)

        def gather_last(e):
            gather(S - 1, C * e, C * (e + 1))
            gather_scales(S - 1, C * e, C * (e + 1))

        for s in range(S):
            quantize(s)
            if s < S - 1:
                gather_early(s, 0, 384)
        for e in range(3):
            gather_last(e)
        for s in range(S - 1):
            gather_early(s, 384, 768)

        def load_w2(e0, e1):
            nc.sync.dma_start(
                out=w2[:, e0:e1, :].bitcast(I32),
                in_=w2_words[e0:e1].rearrange("e s p b -> p (e s) b").bitcast(I32),
            )

        load_w1(1)
        load_w1(2)
        for r in range(4):
            nc.sync.dma_start(
                out=w2s[r:P:32, :, :].bitcast(I32),
                in_=w2_scales.rearrange("e s (b r) i -> r b (e s) i", r=4)[r].bitcast(I32),
            )
        load_w2(0, 6)
        load_w1(3)
        load_w1(4)
        load_w1(5)

        def first(e):
            a = psum_a.tile([P, H], F32, name="a")
            cols = slice(C * e, C * (e + 1))
            for s in range(S):
                nc.tensor.matmul_mx(
                    out=a[:],
                    lhsT=gcodes[s][:, cols].bitcast(E4M3),
                    lhsT_scale=gscales[s][:, cols],
                    rhs=w1[e][:, s, :].bitcast(E2M1),
                    rhs_scale=w1s[:, S * e + s, :],
                    start=(s == 0),
                    stop=(s == S - 1),
                )
            return a

        def relu(e, a):
            r = work.tile([P, 4, P], F32, name="r", align_bytes=64)
            src = a[:].rearrange("c (p t) -> c t p", t=4)
            if e < 4:
                nc.scalar.activation(r[:], src, RELU)
            else:
                nc.vector.tensor_scalar_max(r[:], src, 0.0)
            return r

        def turn(r):
            t = psum_t.tile([P, 4, C], F32, name="t")
            for d in range(4):
                nc.tensor.transpose(t[:, d, :], r[:, d, :], ident[:])
            return t

        def square(t):
            h = work.tile([P, C, 4], BF16, name="h", align_bytes=64)
            nc.scalar.activation(h[:], t[:].rearrange("p t c -> p c t"), SQUARE)
            return h

        def quantize_h(h):
            hc = work.tile([P, C], U32, name="hc", align_bytes=64)
            hs = work.tile([P, C], U8, name="hs", align_bytes=64)
            nc.vector.quantize_mx(out=hc[:].bitcast(E4M3), scales=hs[:], in_=h[:].rearrange("p c t -> p (c t)"))
            return hc, hs

        def second(e, hc, hs):
            b = psum_y.tile([P, N // P, C], F32, name="b")
            for n in range(N // P):
                nc.tensor.matmul_mx(
                    out=b[:, n, :],
                    lhsT=w2[:, e, 2 * P * n : 2 * P * (n + 1)].bitcast(E2M1),
                    lhsT_scale=w2s[:, e, P * n : P * (n + 1)],
                    rhs=hc[:].bitcast(E4M3),
                    rhs_scale=hs[:],
                    start=True,
                    stop=True,
                )
            return b

        def collect(e, b):
            dst = y[:, :, :, e, :]
            src = b[:].rearrange("p n (m u) -> p n m u", m=R)
            nc.vector.tensor_copy(dst, src)

        def store(e0, e1):
            view = out.rearrange("(n p) (m e u) -> p n m e u", p=P, m=R, e=E)
            for n in range(N // P):
                nc.sync.dma_start(
                    out=view[:, n, :, e0:e1, :].rearrange("p m e u -> p m (e u)"),
                    in_=y[:, n, :, e0:e1, :].rearrange("p m e u -> p m (e u)"),
                )

        a, r, t, q, b = {}, {}, {}, {}, {}
        for i in range(E + 2):
            if i < E:
                if i >= 3:
                    gather_last(i)
                a[i] = first(i)
            if 0 <= i - 1 < E:
                t[i - 1] = turn(r[i - 1])
            if 0 <= i - 2 < E:
                b[i - 2] = second(i - 2, *q[i - 2])
            if i < E:
                r[i] = relu(i, a[i])
            if 0 <= i - 1 < E:
                h = square(t[i - 1])
                q[i - 1] = quantize_h(h)
            if 0 <= i - 2 < E:
                collect(i - 2, b[i - 2])
            if i - 2 == 2:
                store(0, 3)
            if i - 2 == 4:
                store(3, 5)
        store(5, 6)
